import numpy as np
import ml_dtypes


def mxq(x, axis, fmt="e4m3"):
    dtype, down = {"e4m3": (ml_dtypes.float8_e4m3fn, 7), "e5m2": (ml_dtypes.float8_e5m2, 14)}[fmt]
    v = np.moveaxis(np.asarray(x, np.float32).astype(ml_dtypes.bfloat16).astype(np.float64), axis, -1)
    blocks = v.reshape(v.shape[:-1] + (-1, 32))
    amax = np.abs(blocks).max(-1, keepdims=True)
    byte = np.maximum(np.where(amax > 0, np.frexp(amax)[1] - 1 + 127, 0) - down, 1)
    scale = np.exp2(byte - 127.0)
    codes = (blocks / scale).astype(np.float32).astype(dtype).astype(np.float64)
    return np.moveaxis((codes * scale).reshape(v.shape), -1, axis)


WIDE = False


def mx_kscale(k):
    if not WIDE:
        return np.ones(k)
    levels = np.array([10, -10, 5, -5, 0])
    if k % 512:
        return np.exp2(np.random.permutation(np.resize(levels, k // 32))).repeat(32)
    a = np.empty((k // 512, 16))
    for p in range(k // 512):
        a[p, :8] = np.random.permutation(np.resize(levels, 8))
        for g in range(8):
            far = levels[np.abs(levels - a[p, g]) >= 10]
            a[p, g + 8] = far[np.random.randint(len(far))]
    return np.exp2(a.ravel()).repeat(32)


def f64(x):
    return np.asarray(x).astype(np.float64)


def striped(idx):
    return np.tile(idx.reshape(-1, 16).T, (8, 1)).astype(np.uint16)


def unstriped(offs):
    return offs[:16].T.reshape(-1).astype(np.int64)


def pack_weight(w):
    k, n = w.shape
    w = f64(np.asarray(w, np.float32).astype(ml_dtypes.bfloat16)).reshape(k // 32, 32, n)
    amax = np.abs(w).max(1)
    byte = np.clip(np.where(amax > 0, np.frexp(amax)[1] - 1 + 127 - 7, 1), 1, 254)
    scaled = (w * np.exp2(127.0 - byte)[:, None, :]).reshape(k, n).astype(np.float32)
    words = np.ascontiguousarray(scaled.reshape(k // 512, 128, 4, n).transpose(0, 1, 3, 2)).astype(ml_dtypes.float8_e4m3fn).view(np.uint8)
    return words, np.ascontiguousarray(byte.astype(np.uint8).reshape(k // 512, 16, n))


def unpack_weight(words, scales):
    g, p, n, _ = words.shape
    vals = np.ascontiguousarray(words).view(ml_dtypes.float8_e4m3fn).astype(np.float64) * np.repeat(np.exp2(scales.astype(np.float64) - 127.0), 8, axis=1)[..., None]
    return vals.transpose(0, 1, 3, 2).reshape(g * 512, n)


K, T, E, C, N = 1536, 512, 8, 128, 128


def by_expert(wq, xq):
    return np.concatenate([wq[e].T @ xq[:, e * C:(e + 1) * C] for e in range(E)], axis=1)


def setup_inputs():
    n = np.random.standard_normal
    s = mx_kscale(K)[:, None]
    first = np.random.permutation(np.repeat(np.arange(E), T // E))
    second = (first + 1 + np.random.permutation(np.repeat(np.arange(E - 1), -(-T // (E - 1)))[:T])) % E
    while np.bincount(second, minlength=E).max() != T // E:
        load = np.bincount(second, minlength=E); hi, lo = int(load.argmax()), int(load.argmin())
        t = np.flatnonzero((second == hi) & (first != lo))[0]; second[t] = lo
    slot_token = np.empty(E * C, np.int64); pos = np.empty((2, T), np.int64); fill = np.zeros(E, np.int64)
    place = np.stack([np.random.permutation(C) for _ in range(E)])
    for r, deal in enumerate((first, second)):
        for t in np.random.permutation(T):
            e = deal[t]; j = e * C + place[e, fill[e]]; fill[e] += 1; slot_token[j] = t; pos[r, t] = j
    g = np.random.uniform(0.2, 0.8, T)
    packed = [pack_weight(m) for m in n((E, K, N)) / np.sqrt(K) / s[None]]
    return {
        "xT": (n((K, T)) * s).astype(np.float32),
        "w_words": np.stack([m[0] for m in packed]),
        "w_scales": np.stack([m[1] for m in packed]),
        "gate": np.stack([np.tile(g, (N, 1)), np.tile(1.0 - g, (N, 1))]).astype(np.float32),
        "offs": striped(slot_token),
        "pos1": striped(pos[0]),
        "pos2": striped(pos[1]),
    }


def reference(xT, w_words, w_scales, gate, offs, pos1, pos2):
    idx = unstriped(offs)
    xq = mxq(f64(xT)[:, idx], 0, "e4m3")
    w = np.stack([unpack_weight(w_words[e], w_scales[e]) for e in range(E)])
    y = by_expert(w, xq)
    return f64(gate[0]) * y[:, unstriped(pos1)] + f64(gate[1]) * y[:, unstriped(pos2)]

from contextlib import ExitStack

import concourse.mybir as mybir

K, T, E, C, N = 1536, 512, 8, 128, 128
SLOTS = E * C
FLOPS = 2 * K * N * SLOTS

F32 = mybir.dt.float32
BF16 = mybir.dt.bfloat16
I32 = mybir.dt.int32
U32 = mybir.dt.uint32
U16 = mybir.dt.uint16
U8 = mybir.dt.uint8
FP8X4 = mybir.dt.float8_e4m3fn_x4
MULT = mybir.AluOpType.mult
ADD = mybir.AluOpType.add

P = 128
PACK = 4
PASSES = K // (P * PACK)
HALF = T // 2

VECTOR_TOKENS = ((160, 160), (0, 64), (0, 0))

GROUPS = ((0, 3), (3, 6), (6, 7), (7, 8))


def tile_routed_moe_kernel(tc, xT, w_words, w_scales, gate, offs, pos1, pos2, out):
    nc = tc.nc
    x_view = xT.rearrange("(g p t) n -> g p t n", p=P, t=PACK)

    with ExitStack() as ctx:
        keep = ctx.enter_context(tc.tile_pool(name="keep", bufs=1))
        psum = ctx.enter_context(tc.psum_pool(name="psum", bufs=1))

        offs_sb = keep.tile([P, SLOTS // 16], U16, name="offs_sb")
        pos1_sb = keep.tile([P, T // 16], U16, name="pos1_sb")
        pos2_sb = keep.tile([P, T // 16], U16, name="pos2_sb")

        warm_in = keep.tile([P, 1], F32, name="warm_in")
        warm_out = keep.tile([P, 1], F32, name="warm_out")
        nc.vector.memset(warm_in[:], 0.0)
        nc.scalar.copy(warm_out[:], warm_in[:])

        x_scales = keep.tile([P, T], U8, name="x_scales", align_bytes=64)
        nc.gpsimd.memset(x_scales[:], 0)
        w_sc = keep.tile([P, E * PASSES * N], U8, name="w_sc", align_bytes=64)
        nc.gpsimd.memset(w_sc[:].bitcast(I32), 0)

        raw = [[keep.tile([P, PACK, HALF], F32, name=f"raw{a}{h}") for h in range(2)] for a in range(PASSES)]

        def load_x(a, h):
            nc.sync.dma_start(out=raw[a][h][:], in_=x_view[a, :, :, h * HALF : (h + 1) * HALF])

        load_x(0, 0)
        load_x(0, 1)
        nc.sync.dma_start(offs_sb[:], offs)
        for a in range(1, PASSES):
            for h in range(2):
                load_x(a, h)
        scale_view = w_scales.bitcast(I32).rearrange("e a q n -> q (e a) n")
        for q in range(4):
            nc.sync.dma_start(
                out=w_sc[32 * q : 32 * q + 4, :].bitcast(I32).rearrange("p (f n) -> p f n", f=E * PASSES),
                in_=scale_view[4 * q : 4 * q + 4],
            )
        w_view = w_words.rearrange("e a p n r -> p (e a) (n r)")
        w_sb = []
        half_blocks = E * PASSES // 2
        for h in range(2):
            w_tile = keep.tile([P, half_blocks * N], I32, name=f"w{h}", align_bytes=64)
            nc.sync.dma_start(
                out=w_tile[:].rearrange("p (f n) -> p f n", f=half_blocks),
                in_=w_view[:, h * half_blocks : (h + 1) * half_blocks, :].bitcast(I32),
            )
            w_sb.append(w_tile)
        nc.sync.dma_start(pos1_sb[:], pos1)
        nc.sync.dma_start(pos2_sb[:], pos2)
        gates = []
        for r in range(2):
            g_tile = keep.tile([P, T], F32, name=f"gate{r}")
            nc.sync.dma_start(out=g_tile[:], in_=gate[r])
            gates.append(g_tile)

        def interleave(copy, grouped, source, lo, hi):
            copy(
                grouped[:, lo:hi, :].rearrange("p (c i) t -> p c t i", i=4),
                source[:, :, lo:hi].rearrange("p t (c i) -> p c t i", i=4),
            )

        words = [keep.tile([P, T], U32, name=f"words{a}", align_bytes=64) for a in range(PASSES)]
        slot_words = [
            [keep.tile([P, (e1 - e0) * C], U32, name=f"sw{a}_{e0}", align_bytes=64) for e0, e1 in GROUPS]
            for a in range(PASSES)
        ]
        slot_scales = [keep.tile([P, (e1 - e0) * C], U8, name=f"ss{e0}", align_bytes=64) for e0, e1 in GROUPS]

        def offsets_of(i):
            e0, e1 = GROUPS[i]
            return offs_sb[:, e0 * C // 16 : e1 * C // 16]

        banks = [psum.tile([P, C], F32, name=f"bank{e}") for e in range(E)]
        results = keep.tile([P, SLOTS], F32, name="results")

        def multiply(a, i):
            e0, e1 = GROUPS[i]
            for e in range(e0, e1):
                block = e * PASSES + a
                w_tile = w_sb[block // half_blocks]
                at = (block % half_blocks) * N
                cols = slice((e - e0) * C, (e - e0 + 1) * C)
                nc.tensor.matmul_mx(
                    out=banks[e][:],
                    lhsT=w_tile[:, at : at + N].bitcast(FP8X4),
                    lhsT_scale=w_sc[:, block * N : (block + 1) * N],
                    rhs=slot_words[a][i][:, cols].bitcast(FP8X4),
                    rhs_scale=slot_scales[i][4 * a : P, cols],
                    start=(a == 0),
                    stop=(a == PASSES - 1),
                )

        for a in range(PASSES):
            for h in range(2):
                grouped = keep.tile([P, HALF, PACK], BF16, name=f"grouped{a}{h}", align_bytes=64)
                v = VECTOR_TOKENS[a][h]
                interleave(nc.scalar.copy, grouped, raw[a][h], v, HALF)
                if v:
                    interleave(nc.vector.tensor_copy, grouped, raw[a][h], 0, v)
                cols = slice(h * HALF, (h + 1) * HALF)
                nc.vector.quantize_mx(
                    out=words[a][:, cols].bitcast(FP8X4),
                    scales=x_scales[4 * a : P, cols],
                    in_=grouped[:].rearrange("p n t -> p (n t)"),
                )
            if a < PASSES - 1:
                for i in range(len(GROUPS)):
                    nc.vector.tensor_copy(slot_words[a][i][:], words[a][:].indirect(offsets_of(i)))

        for i in range(len(GROUPS)):
            nc.vector.tensor_copy(slot_scales[i][:], x_scales[:].indirect(offsets_of(i)))
            for a in range(PASSES - 1):
                multiply(a, i)
        last = PASSES - 1
        for i in range(len(GROUPS)):
            nc.vector.tensor_copy(slot_words[last][i][:], words[last][:].indirect(offsets_of(i)))
            multiply(last, i)
            for e in range(*GROUPS[i]):
                nc.scalar.copy(results[:, e * C : (e + 1) * C], banks[e][:])

        first = keep.tile([P, T], F32, name="first")
        nc.vector.tensor_tensor(first[:], results[:].indirect(pos1_sb[:]), gates[0][:], MULT)
        halves = [slice(0, HALF), slice(HALF, T)]
        second = [keep.tile([P, HALF], F32, name=f"second{h}") for h in range(2)]
        for h in range(2):
            nc.vector.tensor_tensor(
                second[h][:],
                results[:].indirect(pos2_sb[:, h * HALF // 16 : (h + 1) * HALF // 16]),
                gates[1][:, halves[h]],
                MULT,
            )
        for h in range(2):
            total = keep.tile([P, HALF], F32, name=f"total{h}")
            nc.vector.tensor_tensor(total[:], first[:, halves[h]], second[h][:], ADD)
            nc.sync.dma_start(out=out[:, halves[h]], in_=total[:])
